import numpy as np
import ml_dtypes


def mxq(x, axis, fmt="e4m3"):
    dtype, down = {"e4m3": (ml_dtypes.float8_e4m3fn, 7), "e5m2": (ml_dtypes.float8_e5m2, 14)}[fmt]
    v = np.moveaxis(np.asarray(x, np.float32).astype(ml_dtypes.bfloat16).astype(np.float64), axis, -1)
    blocks = v.reshape(v.shape[:-1] + (-1, 32))
    amax = np.abs(blocks).max(-1, keepdims=True)
    byte = np.maximum(np.where(amax > 0, np.frexp(amax)[1] - 1 + 127, 0) - down, 1)
    scale = np.exp2(byte - 127.0)
    codes = (blocks / scale).astype(np.float32).astype(dtype).astype(np.float64)
    return np.moveaxis((codes * scale).reshape(v.shape), -1, axis)


WIDE = False


def mx_kscale(k):
    if not WIDE:
        return np.ones(k)
    levels = np.array([10, -10, 5, -5, 0])
    if k % 512:
        return np.exp2(np.random.permutation(np.resize(levels, k // 32))).repeat(32)
    a = np.empty((k // 512, 16))
    for p in range(k // 512):
        a[p, :8] = np.random.permutation(np.resize(levels, 8))
        for g in range(8):
            far = levels[np.abs(levels - a[p, g]) >= 10]
            a[p, g + 8] = far[np.random.randint(len(far))]
    return np.exp2(a.ravel()).repeat(32)


def f64(x):
    return np.asarray(x).astype(np.float64)


def striped(idx):
    return np.tile(idx.reshape(-1, 16).T, (8, 1)).astype(np.uint16)


def unstriped(offs):
    return offs[:16].T.reshape(-1).astype(np.int64)


def relu(v):
    return np.maximum(v, 0.0)


K, T, E, C, H, N = 512, 512, 4, 256, 1024, 256


def by_expert(wq, xq):
    return np.concatenate([wq[e].T @ xq[:, e * C:(e + 1) * C] for e in range(E)], axis=1)


def setup_inputs():
    n = np.random.standard_normal
    s = mx_kscale(K)[:, None]
    u = mx_kscale(H)
    first = np.random.permutation(np.repeat(np.arange(E), T // E))
    second = (first + 1 + np.random.permutation(np.repeat(np.arange(E - 1), -(-T // (E - 1)))[:T])) % E
    while np.bincount(second, minlength=E).max() != T // E:
        load = np.bincount(second, minlength=E); hi, lo = int(load.argmax()), int(load.argmin())
        t = np.flatnonzero((second == hi) & (first != lo))[0]; second[t] = lo
    slot_token = np.empty(E * C, np.int64); pos = np.empty((2, T), np.int64); fill = np.zeros(E, np.int64)
    place = np.stack([np.random.permutation(C) for _ in range(E)])
    for r, deal in enumerate((first, second)):
        for t in np.random.permutation(T):
            e = deal[t]; j = e * C + place[e, fill[e]]; fill[e] += 1; slot_token[j] = t; pos[r, t] = j
    g = np.random.uniform(0.2, 0.8, T)
    return {
        "xT": (n((K, T)) * s).astype(np.float32),
        "w1": (n((E, K, H)) / np.sqrt(K) / s[None] * u[None, None, :]).astype(np.float32),
        "w2": (n((E, H, N)) / np.sqrt(H) / u[None, :, None]).astype(np.float32),
        "gate": np.stack([np.tile(g, (N, 1)), np.tile(1.0 - g, (N, 1))]).astype(np.float32),
        "offs": striped(slot_token),
        "pos1": striped(pos[0]),
        "pos2": striped(pos[1]),
    }


def reference(xT, w1, w2, gate, offs, pos1, pos2):
    idx = unstriped(offs)
    xq = mxq(f64(xT)[:, idx], 0, "e4m3")
    h = relu(by_expert(mxq(f64(w1), 1, "e4m3"), xq))
    y = by_expert(mxq(f64(w2), 1, "e4m3"), mxq(h, 0, "e4m3"))
    return f64(gate[0]) * y[:, unstriped(pos1)] + f64(gate[1]) * y[:, unstriped(pos2)]

@@ -1,0 +1,219 @@
+from contextlib import ExitStack
+
+import concourse.mybir as mybir
+
+K, T, E, C, H, N = 512, 512, 4, 256, 1024, 256
+FLOPS = 2 * E * C * (K * H + H * N)
+
+F32 = mybir.dt.float32
+BF16 = mybir.dt.bfloat16
+I32 = mybir.dt.int32
+U32 = mybir.dt.uint32
+U16 = mybir.dt.uint16
+U8 = mybir.dt.uint8
+FP8X4 = mybir.dt.float8_e4m3fn_x4
+RELU = mybir.ActivationFunctionType.Relu
+MULT = mybir.AluOpType.mult
+ADD = mybir.AluOpType.add
+
+P = 128
+G = H // 512
+MB = N // P
+S = E * C
+RUN = 8
+WIN = 1536
+
+W1_GROUPS = 512 // RUN
+W2_GROUPS = N // RUN
+W1_SCALAR = {(0, 0): 64, (0, 1): 64, (1, 0): 64, (1, 1): 0, (2, 0): 48, (2, 1): 0, (3, 0): 48, (3, 1): 0}
+W2_SCALAR = {(0, 0): 8, (1, 0): 8, (2, 0): 8, (3, 0): 16, (3, 1): 16}
+XH = 1
+X_SCALAR = 24
+
+
+def tile_routed_moe_kernel(tc, xT, w1, w2, gate, offs, pos1, pos2, out):
+    nc = tc.nc
+    with ExitStack() as ctx:
+        lists = ctx.enter_context(tc.tile_pool(name="lists", bufs=1))
+        keep = ctx.enter_context(tc.tile_pool(name="keep", bufs=1))
+        stage = ctx.enter_context(tc.tile_pool(name="stage", bufs=3))
+        ps1 = ctx.enter_context(tc.psum_pool(name="ps1", bufs=5))
+        ps2 = ctx.enter_context(tc.psum_pool(name="ps2", bufs=3))
+
+        offs_t = lists.tile([P, S // 16], U16, name="offs_t")
+        nc.sync.dma_start(offs_t[:], offs)
+        TH = T // XH
+        xv = xT.rearrange("(p j) t -> p j t", j=4)
+        xraw = []
+        for h in range(XH):
+            xr = keep.tile([P, 4, TH], F32, name="xraw%d" % h)
+            nc.sync.dma_start(xr[:], xv[:, :, h * TH : (h + 1) * TH])
+            xraw.append(xr)
+        w1_pieces = [(e, g, 1) for e in range(E) for g in range(G)]
+        w1raw = {}
+        for e, g0, ng in w1_pieces:
+            w1v = w1[e].rearrange("(p j) c -> p j c", j=4)
+            w1raw[e, g0] = keep.tile([P, 4, ng * 512], F32, name="w1raw%d%d" % (e, g0))
+            nc.sync.dma_start(w1raw[e, g0][:], w1v[:, :, g0 * 512 : (g0 + ng) * 512])
+        pieces = [(e, 0, G) for e in range(E - 1)] + [(E - 1, g, 1) for g in range(G)]
+        w2raw = {}
+        for e, g0, ng in pieces:
+            w2raw[e, g0] = keep.tile([P, ng, 4, N], F32, name="w2raw%d%d" % (e, g0))
+            w2v = w2[e].rearrange("(g p j) n -> p g j n", g=G, j=4)
+            nc.sync.dma_start(w2raw[e, g0][:], w2v[:, g0 : g0 + ng])
+        pos1_t = lists.tile([P, T // 16], U16, name="pos1_t")
+        nc.sync.dma_start(pos1_t[:], pos1)
+        pos2_t = lists.tile([P, T // 16], U16, name="pos2_t")
+        nc.sync.dma_start(pos2_t[:], pos2)
+        pos_t = [pos1_t, pos2_t]
+        gate_t = []
+        for m in range(MB):
+            gt = keep.tile([P, 2, T], F32, name="gate%d" % m)
+            nc.sync.dma_start(gt[:], gate[:, m * P : (m + 1) * P, :].rearrange("r p t -> p r t"))
+            gate_t.append(gt)
+
+        xs = keep.tile([P, WIN], U8, name="xs", align_bytes=64)
+        nc.gpsimd.memset(xs[:], 0)
+        xw = keep.tile([P, WIN], I32, name="xw", align_bytes=64)
+        nc.vector.memset(xw[:, T:WIN], 0)
+        xg = keep.tile([P, T, 4], BF16, name="xg", align_bytes=64)
+        for h in range(XH):
+            dst = xg[:, h * TH : (h + 1) * TH, :].rearrange("p (c i) j -> p c j i", i=RUN)
+            src = xraw[h][:].rearrange("p j (c i) -> p c j i", i=RUN)
+            nc.scalar.copy(out=dst[:, 0:X_SCALAR], in_=src[:, 0:X_SCALAR])
+            nc.vector.tensor_copy(out=dst[:, X_SCALAR:], in_=src[:, X_SCALAR:])
+        nc.vector.quantize_mx(
+            out=xw[:, 0:T].bitcast(FP8X4), scales=xs[:, 0:T], in_=xg[:].rearrange("p t j -> p (t j)")
+        )
+        gw = keep.tile([P, S], U32, name="gw", align_bytes=64)
+        nc.vector.tensor_copy(gw[:], xw[:].bitcast(U32).indirect(offs_t[:]))
+        gs = keep.tile([P, S], U8, name="gs", align_bytes=64)
+        nc.vector.tensor_copy(gs[:], xs[:].indirect(offs_t[:]))
+
+        def shared_copy(dst, src, axis, share):
+            n = dst.shape[axis]
+            if axis == 1:
+                lo, hi = (slice(None), slice(0, share)), (slice(None), slice(share, n))
+            else:
+                lo, hi = (slice(None), slice(None), slice(0, share)), (slice(None), slice(None), slice(share, n))
+            if share > 0:
+                nc.scalar.copy(out=dst[lo], in_=src[lo])
+            if share < n:
+                nc.vector.tensor_copy(out=dst[hi], in_=src[hi])
+
+        w1c = {}
+        w1s = {}
+
+        def prep_w1(e):
+            wg = stage.tile([P, 4, G * 512], BF16, name="wg1", align_bytes=64)
+            for e1, g0, ng in w1_pieces:
+                if e1 == e:
+                    dst = wg[:, :, g0 * 512 : (g0 + ng) * 512].rearrange("p t (a b j) -> p a j b t", b=RUN // 4, j=4)
+                    src = w1raw[e, g0][:].rearrange("p j (a b t) -> p a j b t", b=RUN // 4, t=4)
+                    shared_copy(dst, src, 1, W1_SCALAR[e, g0])
+            w1c[e] = keep.tile([P, 4, G, P], U32, name="w1c%d" % e, align_bytes=64)
+            w1s[e] = keep.tile([P, 4, G, P], U8, name="w1s%d" % e, align_bytes=64)
+            nc.vector.quantize_mx(
+                out=w1c[e][:].rearrange("p t g m -> p (t g m)").bitcast(FP8X4),
+                scales=w1s[e][:].rearrange("p t g m -> p (t g m)"),
+                in_=wg[:].rearrange("p t c -> p (t c)"),
+            )
+
+        hc = {}
+        hs = {}
+
+        def layer1(e):
+            hq = stage.tile([P, G, C, 4], BF16, name="hq", align_bytes=64)
+            for g in range(G):
+                for s in range(C // P):
+                    hps = ps1.tile([P, 4, P], F32, name="hps")
+                    cols = slice(e * C + s * P, e * C + (s + 1) * P)
+                    for t in range(4):
+                        nc.tensor.matmul_mx(
+                            out=hps[:, t, :],
+                            lhsT=w1c[e][:, t, g, :].bitcast(FP8X4),
+                            lhsT_scale=w1s[e][:, t, g, :],
+                            rhs=gw[:, cols].bitcast(FP8X4),
+                            rhs_scale=gs[:, cols],
+                            start=True,
+                            stop=True,
+                        )
+                    nc.scalar.activation(
+                        out=hq[:, g, s * P : (s + 1) * P, :], in_=hps[:].rearrange("p t n -> p n t"), func=RELU
+                    )
+            hc[e] = keep.tile([P, G, C], U32, name="hc%d" % e, align_bytes=64)
+            hs[e] = keep.tile([P, G, C], U8, name="hs%d" % e, align_bytes=64)
+            nc.vector.quantize_mx(
+                out=hc[e][:].rearrange("p g n -> p (g n)").bitcast(FP8X4),
+                scales=hs[e][:].rearrange("p g n -> p (g n)"),
+                in_=hq[:].rearrange("p g n t -> p (g n t)"),
+            )
+
+        w2c = {}
+        w2s = {}
+
+        def prep_w2(e, g0, ng):
+            wg = stage.tile([P, 2048], BF16, name="wg2", align_bytes=64)
+            dst = wg[:, 0 : ng * 4 * N].rearrange("p (g c i j) -> p g c j i", g=ng, i=RUN, j=4)
+            src = w2raw[e, g0][:].rearrange("p g j (c i) -> p g c j i", i=RUN)
+            wc = keep.tile([P, ng * N], U32, name="w2c%d%d" % (e, g0), align_bytes=64)
+            ws = keep.tile([P, ng * N], U8, name="w2s%d%d" % (e, g0), align_bytes=64)
+            if (e, g0) == (E - 1, G - 1):
+                half = W2_GROUPS // 2
+                nc.vector.tensor_copy(out=dst[:, :, 0:half], in_=src[:, :, 0:half])
+                nc.scalar.copy(out=dst[:, :, half:], in_=src[:, :, half:])
+                for m in range(MB):
+                    nc.vector.quantize_mx(
+                        out=wc[:, m * P : (m + 1) * P].bitcast(FP8X4),
+                        scales=ws[:, m * P : (m + 1) * P],
+                        in_=wg[:, m * 4 * P : (m + 1) * 4 * P],
+                    )
+            else:
+                shared_copy(dst, src, 2, W2_SCALAR[e, g0])
+                nc.vector.quantize_mx(out=wc[:].bitcast(FP8X4), scales=ws[:], in_=wg[:, 0 : ng * 4 * N])
+            for g in range(g0, g0 + ng):
+                w2c[e, g] = wc[:, (g - g0) * N : (g - g0 + 1) * N]
+                w2s[e, g] = ws[:, (g - g0) * N : (g - g0 + 1) * N]
+
+        y_sb = [keep.tile([P, S], F32, name="y%d" % m) for m in range(MB)]
+
+        def layer2(e):
+            for m in range(MB):
+                yps = ps2.tile([P, C], F32, name="yps")
+                for g in range(G):
+                    nc.tensor.matmul_mx(
+                        out=yps[:],
+                        lhsT=w2c[e, g][:, m * P : (m + 1) * P].bitcast(FP8X4),
+                        lhsT_scale=w2s[e, g][:, m * P : (m + 1) * P],
+                        rhs=hc[e][:, g, :].bitcast(FP8X4),
+                        rhs_scale=hs[e][:, g, :],
+                        start=(g == 0),
+                        stop=(g == G - 1),
+                    )
+                nc.scalar.copy(out=y_sb[m][:, e * C : (e + 1) * C], in_=yps[:])
+
+        for e in range(E):
+            prep_w1(e)
+            layer1(e)
+        for e, g0, ng in pieces:
+            prep_w2(e, g0, ng)
+            if g0 + ng == G:
+                layer2(e)
+
+        pr = {}
+
+        def fetch(m, r):
+            pr[m, r] = keep.tile([P, T], F32, name="pr%d%d" % (m, r))
+            nc.vector.tensor_tensor(pr[m, r][:], y_sb[m][:].indirect(pos_t[r][:]), gate_t[m][:, r, :], MULT)
+
+        def finish(m):
+            res = keep.tile([P, T], F32, name="res%d" % m)
+            nc.vector.tensor_tensor(res[:], pr[m, 0][:], pr[m, 1][:], ADD)
+            nc.sync.dma_start(out[m * P : (m + 1) * P, :], res[:])
+
+        fetch(0, 0)
+        fetch(0, 1)
+        fetch(1, 0)
+        finish(0)
+        fetch(1, 1)
+        finish(1)

@@ -25,7 +25,7 @@ WIN = 1536
 
 W1_GROUPS = 512 // RUN
 W2_GROUPS = N // RUN
-W1_SCALAR = {(0, 0): 64, (0, 1): 64, (1, 0): 64, (1, 1): 0, (2, 0): 48, (2, 1): 0, (3, 0): 48, (3, 1): 0}
+W1_SCALAR = {(0, 0): 80, (1, 0): 64, (1, 1): 0, (2, 0): 48, (2, 1): 0, (3, 0): 48, (3, 1): 0}
 W2_SCALAR = {(0, 0): 8, (1, 0): 8, (2, 0): 8, (3, 0): 16, (3, 1): 16}
 XH = 1
 X_SCALAR = 24
@@ -49,7 +49,7 @@ def tile_routed_moe_kernel(tc, xT, w1, w2, gate, offs, pos1, pos2, out):
             xr = keep.tile([P, 4, TH], F32, name="xraw%d" % h)
             nc.sync.dma_start(xr[:], xv[:, :, h * TH : (h + 1) * TH])
             xraw.append(xr)
-        w1_pieces = [(e, g, 1) for e in range(E) for g in range(G)]
+        w1_pieces = [(0, 0, 2)] + [(e, g, 1) for e in range(1, E) for g in range(G)]
         w1raw = {}
         for e, g0, ng in w1_pieces:
             w1v = w1[e].rearrange("(p j) c -> p j c", j=4)

@@ -25,7 +25,7 @@ WIN = 1536
 
 W1_GROUPS = 512 // RUN
 W2_GROUPS = N // RUN
-W1_SCALAR = {(0, 0): 80, (1, 0): 64, (1, 1): 0, (2, 0): 48, (2, 1): 0, (3, 0): 48, (3, 1): 0}
+W1_SCALAR = {(0, 0): 80, (1, 0): 64, (1, 1): 0, (2, 0): 0, (3, 0): 48, (3, 1): 0}
 W2_SCALAR = {(0, 0): 8, (1, 0): 8, (2, 0): 8, (3, 0): 16, (3, 1): 16}
 XH = 1
 X_SCALAR = 24
@@ -49,7 +49,7 @@ def tile_routed_moe_kernel(tc, xT, w1, w2, gate, offs, pos1, pos2, out):
             xr = keep.tile([P, 4, TH], F32, name="xraw%d" % h)
             nc.sync.dma_start(xr[:], xv[:, :, h * TH : (h + 1) * TH])
             xraw.append(xr)
-        w1_pieces = [(0, 0, 2)] + [(e, g, 1) for e in range(1, E) for g in range(G)]
+        w1_pieces = [(0, 0, 2), (1, 0, 1), (1, 1, 1), (2, 0, 2), (3, 0, 1), (3, 1, 1)]
         w1raw = {}
         for e, g0, ng in w1_pieces:
             w1v = w1[e].rearrange("(p j) c -> p j c", j=4)

@@ -25,7 +25,7 @@ WIN = 1536
 
 W1_GROUPS = 512 // RUN
 W2_GROUPS = N // RUN
-W1_SCALAR = {(0, 0): 80, (1, 0): 64, (1, 1): 0, (2, 0): 0, (3, 0): 48, (3, 1): 0}
+W1_SCALAR = {(0, 0): 80, (1, 0): 64, (1, 1): 0, (2, 0): 0, (3, 0): 64, (3, 1): 0}
 W2_SCALAR = {(0, 0): 8, (1, 0): 8, (2, 0): 8, (3, 0): 16, (3, 1): 16}
 XH = 1
 X_SCALAR = 24
@@ -40,8 +40,6 @@ def tile_routed_moe_kernel(tc, xT, w1, w2, gate, offs, pos1, pos2, out):
         ps1 = ctx.enter_context(tc.psum_pool(name="ps1", bufs=5))
         ps2 = ctx.enter_context(tc.psum_pool(name="ps2", bufs=3))
 
-        offs_t = lists.tile([P, S // 16], U16, name="offs_t")
-        nc.sync.dma_start(offs_t[:], offs)
         TH = T // XH
         xv = xT.rearrange("(p j) t -> p j t", j=4)
         xraw = []
@@ -49,6 +47,8 @@ def tile_routed_moe_kernel(tc, xT, w1, w2, gate, offs, pos1, pos2, out):
             xr = keep.tile([P, 4, TH], F32, name="xraw%d" % h)
             nc.sync.dma_start(xr[:], xv[:, :, h * TH : (h + 1) * TH])
             xraw.append(xr)
+        offs_t = lists.tile([P, S // 16], U16, name="offs_t")
+        nc.sync.dma_start(offs_t[:], offs)
         w1_pieces = [(0, 0, 2), (1, 0, 1), (1, 1, 1), (2, 0, 2), (3, 0, 1), (3, 1, 1)]
         w1raw = {}
         for e, g0, ng in w1_pieces:

@@ -25,7 +25,7 @@ WIN = 1536
 
 W1_GROUPS = 512 // RUN
 W2_GROUPS = N // RUN
-W1_SCALAR = {(0, 0): 80, (1, 0): 64, (1, 1): 0, (2, 0): 0, (3, 0): 64, (3, 1): 0}
+W1_SCALAR = {(0, 0): 96, (1, 0): 48, (2, 0): 0, (3, 0): 64, (3, 1): 0}
 W2_SCALAR = {(0, 0): 8, (1, 0): 8, (2, 0): 8, (3, 0): 16, (3, 1): 16}
 XH = 1
 X_SCALAR = 24
@@ -49,18 +49,20 @@ def tile_routed_moe_kernel(tc, xT, w1, w2, gate, offs, pos1, pos2, out):
             xraw.append(xr)
         offs_t = lists.tile([P, S // 16], U16, name="offs_t")
         nc.sync.dma_start(offs_t[:], offs)
-        w1_pieces = [(0, 0, 2), (1, 0, 1), (1, 1, 1), (2, 0, 2), (3, 0, 1), (3, 1, 1)]
+        loads = [(1, 0, 0, 2), (1, 1, 0, 2), (1, 2, 0, 2), (1, 3, 0, 1), (1, 3, 1, 1), (2, 0, 0, 2), (2, 1, 0, 2), (2, 2, 0, 2), (2, 3, 0, 1), (2, 3, 1, 1)]
+        w1_pieces = [(e, g0, ng) for w, e, g0, ng in loads if w == 1]
+        pieces = [(e, g0, ng) for w, e, g0, ng in loads if w == 2]
         w1raw = {}
-        for e, g0, ng in w1_pieces:
-            w1v = w1[e].rearrange("(p j) c -> p j c", j=4)
-            w1raw[e, g0] = keep.tile([P, 4, ng * 512], F32, name="w1raw%d%d" % (e, g0))
-            nc.sync.dma_start(w1raw[e, g0][:], w1v[:, :, g0 * 512 : (g0 + ng) * 512])
-        pieces = [(e, 0, G) for e in range(E - 1)] + [(E - 1, g, 1) for g in range(G)]
         w2raw = {}
-        for e, g0, ng in pieces:
-            w2raw[e, g0] = keep.tile([P, ng, 4, N], F32, name="w2raw%d%d" % (e, g0))
-            w2v = w2[e].rearrange("(g p j) n -> p g j n", g=G, j=4)
-            nc.sync.dma_start(w2raw[e, g0][:], w2v[:, g0 : g0 + ng])
+        for w, e, g0, ng in loads:
+            if w == 1:
+                w1v = w1[e].rearrange("(p j) c -> p j c", j=4)
+                w1raw[e, g0] = keep.tile([P, 4, ng * 512], F32, name="w1raw%d%d" % (e, g0))
+                nc.sync.dma_start(w1raw[e, g0][:], w1v[:, :, g0 * 512 : (g0 + ng) * 512])
+            else:
+                w2raw[e, g0] = keep.tile([P, ng, 4, N], F32, name="w2raw%d%d" % (e, g0))
+                w2v = w2[e].rearrange("(g p j) n -> p g j n", g=G, j=4)
+                nc.sync.dma_start(w2raw[e, g0][:], w2v[:, g0 : g0 + ng])
         pos1_t = lists.tile([P, T // 16], U16, name="pos1_t")
         nc.sync.dma_start(pos1_t[:], pos1)
         pos2_t = lists.tile([P, T // 16], U16, name="pos2_t")

@@ -1,6 +1,7 @@
 from contextlib import ExitStack
 
 import concourse.mybir as mybir
+from concourse.masks import make_identity
 
 K, T, E, C, H, N = 512, 512, 4, 256, 1024, 256
 FLOPS = 2 * E * C * (K * H + H * N)
@@ -27,6 +28,7 @@ W1_GROUPS = 512 // RUN
 W2_GROUPS = N // RUN
 W1_SCALAR = {(0, 0): 96, (1, 0): 48, (2, 0): 0, (3, 0): 64, (3, 1): 0}
 W2_SCALAR = {(0, 0): 8, (1, 0): 8, (2, 0): 8, (3, 0): 16, (3, 1): 16}
+PE_ADD = 256
 XH = 1
 X_SCALAR = 24
 
@@ -202,6 +204,8 @@ def tile_routed_moe_kernel(tc, xT, w1, w2, gate, offs, pos1, pos2, out):
             if g0 + ng == G:
                 layer2(e)
 
+        ident = keep.tile([P, P], F32, name="ident")
+        make_identity(nc, ident[:])
         pr = {}
 
         def fetch(m, r):
@@ -210,7 +214,13 @@ def tile_routed_moe_kernel(tc, xT, w1, w2, gate, offs, pos1, pos2, out):
 
         def finish(m):
             res = keep.tile([P, T], F32, name="res%d" % m)
-            nc.vector.tensor_tensor(res[:], pr[m, 0][:], pr[m, 1][:], ADD)
+            split = PE_ADD if m == 0 else 0
+            if split > 0:
+                both = ps2.tile([P, split], F32, name="yps")
+                for r in range(2):
+                    nc.tensor.matmul(out=both[:], lhsT=ident[:], rhs=pr[m, r][:, 0:split], start=(r == 0), stop=(r == 1))
+                nc.scalar.copy(out=res[:, 0:split], in_=both[:])
+            nc.vector.tensor_tensor(res[:, split:T], pr[m, 0][:, split:T], pr[m, 1][:, split:T], ADD)
             nc.sync.dma_start(out[m * P : (m + 1) * P, :], res[:])
 
         fetch(0, 0)

from contextlib import ExitStack

import concourse.mybir as mybir
from concourse.masks import make_identity

K, T, E, C, H, N = 512, 512, 4, 256, 1024, 256
FLOPS = 2 * E * C * (K * H + H * N)

F32 = mybir.dt.float32
BF16 = mybir.dt.bfloat16
I32 = mybir.dt.int32
U32 = mybir.dt.uint32
U16 = mybir.dt.uint16
U8 = mybir.dt.uint8
FP8X4 = mybir.dt.float8_e4m3fn_x4
RELU = mybir.ActivationFunctionType.Relu
MULT = mybir.AluOpType.mult
ADD = mybir.AluOpType.add

P = 128
G = H // 512
MB = N // P
S = E * C
RUN = 8
WIN = 1536

W1_GROUPS = 512 // RUN
W2_GROUPS = N // RUN
W1_SCALAR = {(0, 0): 96, (1, 0): 48, (2, 0): 0, (3, 0): 64, (3, 1): 0}
W2_SCALAR = {(0, 0): 8, (1, 0): 8, (2, 0): 8, (3, 0): 16, (3, 1): 16}
PE_ADD = 256
XH = 1
X_SCALAR = 24


def tile_routed_moe_kernel(tc, xT, w1, w2, gate, offs, pos1, pos2, out):
    nc = tc.nc
    with ExitStack() as ctx:
        lists = ctx.enter_context(tc.tile_pool(name="lists", bufs=1))
        keep = ctx.enter_context(tc.tile_pool(name="keep", bufs=1))
        stage = ctx.enter_context(tc.tile_pool(name="stage", bufs=3))
        ps1 = ctx.enter_context(tc.psum_pool(name="ps1", bufs=5))
        ps2 = ctx.enter_context(tc.psum_pool(name="ps2", bufs=3))

        TH = T // XH
        xv = xT.rearrange("(p j) t -> p j t", j=4)
        xraw = []
        for h in range(XH):
            xr = keep.tile([P, 4, TH], F32, name="xraw%d" % h)
            nc.sync.dma_start(xr[:], xv[:, :, h * TH : (h + 1) * TH])
            xraw.append(xr)
        offs_t = lists.tile([P, S // 16], U16, name="offs_t")
        nc.sync.dma_start(offs_t[:], offs)
        loads = [(1, 0, 0, 2), (1, 1, 0, 2), (1, 2, 0, 2), (1, 3, 0, 1), (1, 3, 1, 1), (2, 0, 0, 2), (2, 1, 0, 2), (2, 2, 0, 2), (2, 3, 0, 1), (2, 3, 1, 1)]
        w1_pieces = [(e, g0, ng) for w, e, g0, ng in loads if w == 1]
        pieces = [(e, g0, ng) for w, e, g0, ng in loads if w == 2]
        w1raw = {}
        w2raw = {}
        for w, e, g0, ng in loads:
            if w == 1:
                w1v = w1[e].rearrange("(p j) c -> p j c", j=4)
                w1raw[e, g0] = keep.tile([P, 4, ng * 512], F32, name="w1raw%d%d" % (e, g0))
                nc.sync.dma_start(w1raw[e, g0][:], w1v[:, :, g0 * 512 : (g0 + ng) * 512])
            else:
                w2raw[e, g0] = keep.tile([P, ng, 4, N], F32, name="w2raw%d%d" % (e, g0))
                w2v = w2[e].rearrange("(g p j) n -> p g j n", g=G, j=4)
                nc.sync.dma_start(w2raw[e, g0][:], w2v[:, g0 : g0 + ng])
        pos1_t = lists.tile([P, T // 16], U16, name="pos1_t")
        nc.sync.dma_start(pos1_t[:], pos1)
        pos2_t = lists.tile([P, T // 16], U16, name="pos2_t")
        nc.sync.dma_start(pos2_t[:], pos2)
        pos_t = [pos1_t, pos2_t]
        gate_t = []
        for m in range(MB):
            gt = keep.tile([P, 2, T], F32, name="gate%d" % m)
            nc.sync.dma_start(gt[:], gate[:, m * P : (m + 1) * P, :].rearrange("r p t -> p r t"))
            gate_t.append(gt)

        xs = keep.tile([P, WIN], U8, name="xs", align_bytes=64)
        nc.gpsimd.memset(xs[:], 0)
        xw = keep.tile([P, WIN], I32, name="xw", align_bytes=64)
        nc.vector.memset(xw[:, T:WIN], 0)
        xg = keep.tile([P, T, 4], BF16, name="xg", align_bytes=64)
        for h in range(XH):
            dst = xg[:, h * TH : (h + 1) * TH, :].rearrange("p (c i) j -> p c j i", i=RUN)
            src = xraw[h][:].rearrange("p j (c i) -> p c j i", i=RUN)
            nc.scalar.copy(out=dst[:, 0:X_SCALAR], in_=src[:, 0:X_SCALAR])
            nc.vector.tensor_copy(out=dst[:, X_SCALAR:], in_=src[:, X_SCALAR:])
        nc.vector.quantize_mx(
            out=xw[:, 0:T].bitcast(FP8X4), scales=xs[:, 0:T], in_=xg[:].rearrange("p t j -> p (t j)")
        )
        gw = keep.tile([P, S], U32, name="gw", align_bytes=64)
        nc.vector.tensor_copy(gw[:], xw[:].bitcast(U32).indirect(offs_t[:]))
        gs = keep.tile([P, S], U8, name="gs", align_bytes=64)
        nc.vector.tensor_copy(gs[:], xs[:].indirect(offs_t[:]))

        def shared_copy(dst, src, axis, share):
            n = dst.shape[axis]
            if axis == 1:
                lo, hi = (slice(None), slice(0, share)), (slice(None), slice(share, n))
            else:
                lo, hi = (slice(None), slice(None), slice(0, share)), (slice(None), slice(None), slice(share, n))
            if share > 0:
                nc.scalar.copy(out=dst[lo], in_=src[lo])
            if share < n:
                nc.vector.tensor_copy(out=dst[hi], in_=src[hi])

        w1c = {}
        w1s = {}

        def prep_w1(e):
            wg = stage.tile([P, 4, G * 512], BF16, name="wg1", align_bytes=64)
            for e1, g0, ng in w1_pieces:
                if e1 == e:
                    dst = wg[:, :, g0 * 512 : (g0 + ng) * 512].rearrange("p t (a b j) -> p a j b t", b=RUN // 4, j=4)
                    src = w1raw[e, g0][:].rearrange("p j (a b t) -> p a j b t", b=RUN // 4, t=4)
                    shared_copy(dst, src, 1, W1_SCALAR[e, g0])
            w1c[e] = keep.tile([P, 4, G, P], U32, name="w1c%d" % e, align_bytes=64)
            w1s[e] = keep.tile([P, 4, G, P], U8, name="w1s%d" % e, align_bytes=64)
            nc.vector.quantize_mx(
                out=w1c[e][:].rearrange("p t g m -> p (t g m)").bitcast(FP8X4),
                scales=w1s[e][:].rearrange("p t g m -> p (t g m)"),
                in_=wg[:].rearrange("p t c -> p (t c)"),
            )

        hc = {}
        hs = {}

        def layer1(e):
            hq = stage.tile([P, G, C, 4], BF16, name="hq", align_bytes=64)
            for g in range(G):
                for s in range(C // P):
                    hps = ps1.tile([P, 4, P], F32, name="hps")
                    cols = slice(e * C + s * P, e * C + (s + 1) * P)
                    for t in range(4):
                        nc.tensor.matmul_mx(
                            out=hps[:, t, :],
                            lhsT=w1c[e][:, t, g, :].bitcast(FP8X4),
                            lhsT_scale=w1s[e][:, t, g, :],
                            rhs=gw[:, cols].bitcast(FP8X4),
                            rhs_scale=gs[:, cols],
                            start=True,
                            stop=True,
                        )
                    nc.scalar.activation(
                        out=hq[:, g, s * P : (s + 1) * P, :], in_=hps[:].rearrange("p t n -> p n t"), func=RELU
                    )
            hc[e] = keep.tile([P, G, C], U32, name="hc%d" % e, align_bytes=64)
            hs[e] = keep.tile([P, G, C], U8, name="hs%d" % e, align_bytes=64)
            nc.vector.quantize_mx(
                out=hc[e][:].rearrange("p g n -> p (g n)").bitcast(FP8X4),
                scales=hs[e][:].rearrange("p g n -> p (g n)"),
                in_=hq[:].rearrange("p g n t -> p (g n t)"),
            )

        w2c = {}
        w2s = {}

        def prep_w2(e, g0, ng):
            wg = stage.tile([P, 2048], BF16, name="wg2", align_bytes=64)
            dst = wg[:, 0 : ng * 4 * N].rearrange("p (g c i j) -> p g c j i", g=ng, i=RUN, j=4)
            src = w2raw[e, g0][:].rearrange("p g j (c i) -> p g c j i", i=RUN)
            wc = keep.tile([P, ng * N], U32, name="w2c%d%d" % (e, g0), align_bytes=64)
            ws = keep.tile([P, ng * N], U8, name="w2s%d%d" % (e, g0), align_bytes=64)
            if (e, g0) == (E - 1, G - 1):
                half = W2_GROUPS // 2
                nc.vector.tensor_copy(out=dst[:, :, 0:half], in_=src[:, :, 0:half])
                nc.scalar.copy(out=dst[:, :, half:], in_=src[:, :, half:])
                for m in range(MB):
                    nc.vector.quantize_mx(
                        out=wc[:, m * P : (m + 1) * P].bitcast(FP8X4),
                        scales=ws[:, m * P : (m + 1) * P],
                        in_=wg[:, m * 4 * P : (m + 1) * 4 * P],
                    )
            else:
                shared_copy(dst, src, 2, W2_SCALAR[e, g0])
                nc.vector.quantize_mx(out=wc[:].bitcast(FP8X4), scales=ws[:], in_=wg[:, 0 : ng * 4 * N])
            for g in range(g0, g0 + ng):
                w2c[e, g] = wc[:, (g - g0) * N : (g - g0 + 1) * N]
                w2s[e, g] = ws[:, (g - g0) * N : (g - g0 + 1) * N]

        y_sb = [keep.tile([P, S], F32, name="y%d" % m) for m in range(MB)]

        def layer2(e):
            for m in range(MB):
                yps = ps2.tile([P, C], F32, name="yps")
                for g in range(G):
                    nc.tensor.matmul_mx(
                        out=yps[:],
                        lhsT=w2c[e, g][:, m * P : (m + 1) * P].bitcast(FP8X4),
                        lhsT_scale=w2s[e, g][:, m * P : (m + 1) * P],
                        rhs=hc[e][:, g, :].bitcast(FP8X4),
                        rhs_scale=hs[e][:, g, :],
                        start=(g == 0),
                        stop=(g == G - 1),
                    )
                nc.scalar.copy(out=y_sb[m][:, e * C : (e + 1) * C], in_=yps[:])

        for e in range(E):
            prep_w1(e)
            layer1(e)
        for e, g0, ng in pieces:
            prep_w2(e, g0, ng)
            if g0 + ng == G:
                layer2(e)

        ident = keep.tile([P, P], F32, name="ident")
        make_identity(nc, ident[:])
        pr = {}

        def fetch(m, r):
            pr[m, r] = keep.tile([P, T], F32, name="pr%d%d" % (m, r))
            nc.vector.tensor_tensor(pr[m, r][:], y_sb[m][:].indirect(pos_t[r][:]), gate_t[m][:, r, :], MULT)

        def finish(m):
            res = keep.tile([P, T], F32, name="res%d" % m)
            split = PE_ADD if m == 0 else 0
            if split > 0:
                both = ps2.tile([P, split], F32, name="yps")
                for r in range(2):
                    nc.tensor.matmul(out=both[:], lhsT=ident[:], rhs=pr[m, r][:, 0:split], start=(r == 0), stop=(r == 1))
                nc.scalar.copy(out=res[:, 0:split], in_=both[:])
            nc.vector.tensor_tensor(res[:, split:T], pr[m, 0][:, split:T], pr[m, 1][:, split:T], ADD)
            nc.sync.dma_start(out[m * P : (m + 1) * P, :], res[:])

        fetch(0, 0)
        fetch(0, 1)
        fetch(1, 0)
        finish(0)
        fetch(1, 1)
        finish(1)
